import numpy as np
import ml_dtypes


def mxq(x, axis, fmt="e4m3"):
    dtype, down = {"e4m3": (ml_dtypes.float8_e4m3fn, 7), "e5m2": (ml_dtypes.float8_e5m2, 14)}[fmt]
    v = np.moveaxis(np.asarray(x, np.float32).astype(ml_dtypes.bfloat16).astype(np.float64), axis, -1)
    blocks = v.reshape(v.shape[:-1] + (-1, 32))
    amax = np.abs(blocks).max(-1, keepdims=True)
    byte = np.maximum(np.where(amax > 0, np.frexp(amax)[1] - 1 + 127, 0) - down, 1)
    scale = np.exp2(byte - 127.0)
    codes = (blocks / scale).astype(np.float32).astype(dtype).astype(np.float64)
    return np.moveaxis((codes * scale).reshape(v.shape), -1, axis)


WIDE = False


def mx_kscale(k):
    if not WIDE:
        return np.ones(k)
    levels = np.array([30, -30])
    if k % 512:
        return np.exp2(np.random.permutation(np.resize(levels, k // 32))).repeat(32)
    a = np.empty((k // 512, 16))
    for p in range(k // 512):
        a[p, :8] = np.random.permutation(np.resize(levels, 8))
        for g in range(8):
            far = levels[np.abs(levels - a[p, g]) >= 10]
            a[p, g + 8] = far[np.random.randint(len(far))]
    return np.exp2(a.ravel()).repeat(32)


def f64(x):
    return np.asarray(x).astype(np.float64)


def striped(idx):
    return np.tile(np.asarray(idx).reshape(-1, 16).T, (8, 1)).astype(np.uint16)


def unstriped(offs):
    return offs[:16].T.reshape(-1).astype(np.int64)


E2M1 = np.array([0.0, 0.5, 1.0, 1.5, 2.0, 3.0, 4.0, 6.0, -0.0, -0.5, -1.0, -1.5, -2.0, -3.0, -4.0, -6.0])


def pack_weight(w, fmt):
    k, n = w.shape
    w = f64(np.asarray(w, np.float32).astype(ml_dtypes.bfloat16)).reshape(k // 32, 32, n)
    amax = np.abs(w).max(1)
    if fmt in ("e4m3", "e5m2"):
        byte = np.frexp(amax)[1] - 1 + 127 - (7 if fmt == "e4m3" else 14)
    else:
        mant, ex = np.frexp(amax / 6.0)
        byte = np.where(mant > 0.5, ex, ex - 1) + 127
    byte = np.clip(np.where(amax > 0, byte, 1), 1, 254)
    scaled = (w * np.exp2(127.0 - byte)[:, None, :]).reshape(k, n).astype(np.float32)
    by_word = np.ascontiguousarray(scaled.reshape(k // 512, 128, 4, n).transpose(0, 1, 3, 2))
    if fmt in ("e4m3", "e5m2"):
        words = by_word.astype(ml_dtypes.float8_e4m3fn if fmt == "e4m3" else ml_dtypes.float8_e5m2).view(np.uint8)
    else:
        c = by_word.astype(ml_dtypes.float4_e2m1fn).view(np.uint8) & 0xF
        words = (c[..., 0::2] | (c[..., 1::2] << 4)).reshape(k // 512, 128, 2 * n)
    return np.ascontiguousarray(words), np.ascontiguousarray(byte.astype(np.uint8).reshape(k // 512, 16, n))


def unpack_weight(words, scales, fmt):
    g, _, n = scales.shape
    words = np.ascontiguousarray(words).reshape(g, 128, n, -1)
    if fmt in ("e4m3", "e5m2"):
        vals = words.view(ml_dtypes.float8_e4m3fn if fmt == "e4m3" else ml_dtypes.float8_e5m2).astype(np.float64)
    else:
        nib = np.empty((g, 128, n, 4), np.uint8)
        nib[..., 0::2] = words & 0xF
        nib[..., 1::2] = words >> 4
        vals = E2M1[nib]
    vals = vals * np.repeat(np.exp2(scales.astype(np.float64) - 127.0), 8, axis=1)[..., None]
    return vals.transpose(0, 1, 3, 2).reshape(g * 512, n)


K, J, N, R, T = 512, 512, 256, 256, 1024


def setup_inputs():
    n = np.random.standard_normal
    idx = np.random.permutation(T)[:J]
    idx2 = np.random.permutation(T)[:J]
    fj = mx_kscale(J)
    fk = mx_kscale(K)
    gjp = pack_weight(n((J, N)) * np.exp(0.5 * n((J, 1))) / fj[:, None], "e5m2")
    drp = pack_weight(n((K, R)) * 1 / np.sqrt(K) / fk[:, None], "e2m1")
    return {
        "xf": (n((K, T))).astype(np.float32),
        "ra": (np.random.uniform(0.5, 1.5, (1, J)) * fj).astype(np.float32),
        "gj_words": gjp[0],
        "gj_scales": gjp[1],
        "fkr": (np.random.uniform(0.5, 1.5, (1, K)) * fk).astype(np.float32),
        "dr_words": drp[0],
        "dr_scales": drp[1],
        "bn": (np.random.uniform(-12.0, 12.0, (1, N))).astype(np.float32),
        "offs": striped(idx),
        "offs2": striped(idx2),
    }


def reference(xf, ra, gj_words, gj_scales, fkr, dr_words, dr_scales, bn, offs, offs2):
    idx = unstriped(offs)
    idx2 = unstriped(offs2)
    gju = unpack_weight(gj_words, gj_scales, "e5m2")
    dru = unpack_weight(dr_words, dr_scales, "e2m1")
    us = np.maximum(f64(xf)[:, idx], f64(xf)[:, idx2]) * f64(ra)
    ut = us.T
    uj = ut * f64(fkr)
    ujq = mxq(uj, 0, "e5m2")
    w = ujq.T @ gju
    wq = mxq(w, 0, "e5m2")
    v2 = dru.T @ wq
    wv = v2 + f64(bn)
    mn = np.mean(wv, axis=1, keepdims=True)
    dw = wv - mn
    y = dw / (np.mean(np.abs(dw), axis=1, keepdims=True) + 2.0)
    return y

@@ -1,0 +1,187 @@
+from contextlib import ExitStack
+
+import concourse.mybir as mybir
+from concourse.masks import make_identity
+
+K, J, N, R, T = 512, 512, 256, 256, 1024
+FLOPS = 2 * J * K * N + 2 * K * R * N
+
+F32 = mybir.dt.float32
+BF16 = mybir.dt.bfloat16
+I32 = mybir.dt.int32
+U32 = mybir.dt.uint32
+U16 = mybir.dt.uint16
+U8 = mybir.dt.uint8
+E5M2X4 = mybir.dt.float8_e5m2_x4
+E2M1X4 = mybir.dt.float4_e2m1fn_x4
+ALU = mybir.AluOpType
+ACT = mybir.ActivationFunctionType
+
+P = 128
+PACK = 4
+
+
+def tile_list_directions_larger_stored_spread_kernel(
+    tc, xf, ra, gj_words, gj_scales, fkr, dr_words, dr_scales, bn, offs, offs2, out
+):
+    nc = tc.nc
+    with ExitStack() as ctx:
+        keep = ctx.enter_context(tc.tile_pool(name="keep", bufs=1))
+        psum = ctx.enter_context(tc.psum_pool(name="psum", bufs=1))
+
+        list_a = keep.tile([P, J // 16], U16, name="list_a")
+        list_b = keep.tile([P, J // 16], U16, name="list_b")
+        rows = xf.rearrange("(p t) c -> t p c", t=PACK)
+        x_sb = [keep.tile([P, T], F32, name=f"x{t}") for t in range(PACK)]
+        ra_sb = keep.tile([P, PACK], F32, name="ra_sb")
+        fk_sb = keep.tile([P, PACK], F32, name="fk_sb")
+
+        nc.sync.dma_start(out=x_sb[0][:], in_=rows[0])
+        nc.sync.dma_start(list_a[:], offs)
+        nc.sync.dma_start(list_b[:], offs2)
+        nc.scalar.dma_start(out=ra_sb[:], in_=ra.rearrange("o (p t) -> (o p) t", t=PACK))
+        nc.scalar.dma_start(out=fk_sb[:], in_=fkr.rearrange("o (p t) -> (o p) t", t=PACK))
+        for t in range(1, PACK):
+            nc.sync.dma_start(out=x_sb[t][:], in_=rows[t])
+
+        gj_sc = keep.tile([P, N], U8, name="gj_sc", align_bytes=64)
+        dr_sc = keep.tile([P, R], U8, name="dr_sc", align_bytes=64)
+        nc.gpsimd.memset(gj_sc[:].bitcast(I32), 0)
+        nc.gpsimd.memset(dr_sc[:].bitcast(I32), 0)
+        ident = keep.tile([P, P], F32, name="ident")
+        make_identity(nc, ident[:])
+
+        gj_w = keep.tile([P, N], U32, name="gj_w", align_bytes=64)
+        dr_w = keep.tile([P, 2 * R], U8, name="dr_w", align_bytes=64)
+        bn_sb = keep.tile([P, N], F32, name="bn_sb")
+        nc.sync.dma_start(out=gj_w[:].bitcast(I32), in_=gj_words[0].rearrange("p n t -> p (n t)").bitcast(I32))
+        for q in range(4):
+            nc.sync.dma_start(out=gj_sc[32 * q : 32 * q + 4, :].bitcast(I32), in_=gj_scales[0, 4 * q : 4 * q + 4, :].bitcast(I32))
+        nc.sync.dma_start(out=dr_w[:].bitcast(I32), in_=dr_words[0].bitcast(I32))
+        for q in range(4):
+            nc.sync.dma_start(out=dr_sc[32 * q : 32 * q + 4, :].bitcast(I32), in_=dr_scales[0, 4 * q : 4 * q + 4, :].bitcast(I32))
+        nc.sync.dma_start(out=bn_sb[:], in_=bn[0].partition_broadcast(P))
+
+        ra_ps = psum.tile([P, PACK, P], F32, name="ra_ps")
+        for t in range(PACK):
+            nc.tensor.transpose(ra_ps[:, t, :], ra_sb[:, t : t + 1].to_broadcast([P, P]), ident[:])
+
+        ga = [keep.tile([P, J], F32, name=f"ga{t}") for t in range(PACK)]
+        gb = [keep.tile([P, J], F32, name=f"gb{t}") for t in range(PACK)]
+        big = [keep.tile([P, J], F32, name=f"big{t}") for t in range(PACK)]
+        u_kj = [keep.tile([P, J], BF16, name=f"u_kj{t}") for t in range(PACK)]
+        u_ps = [psum.tile([P, 2, P], F32, name=f"u_ps{t}", tag=f"u_ps{t % 3}") for t in range(PACK)]
+        u_jk = [keep.tile([P, P * PACK], BF16, name=f"u_jk{t}", align_bytes=64) for t in range(PACK)]
+        u_w = [keep.tile([P, P], U32, name=f"u_w{t}", align_bytes=64) for t in range(PACK)]
+        u_sc = [keep.tile([P, P], U8, name=f"u_sc{t}", align_bytes=64) for t in range(PACK)]
+        w_ps = [psum.tile([P, PACK, P], F32, name=f"w_ps{h}") for h in range(2)]
+
+        def gather_v(dst, t, lst, c0, c1):
+            nc.vector.tensor_copy(dst[:, 16 * c0 : 16 * c1], x_sb[t][:].indirect(lst[:, c0:c1]))
+
+        def gather_s(dst, t, lst, c0, c1):
+            nc.scalar.activation(dst[:, 16 * c0 : 16 * c1], x_sb[t][:].indirect(lst[:, c0:c1]), ACT.Copy)
+
+        def combine(t):
+            nc.vector.tensor_tensor(big[t][:], ga[t][:], gb[t][:], ALU.max)
+
+        def weigh(t):
+            nc.vector.scalar_tensor_tensor(
+                out=u_kj[t][:].rearrange("p (q t) -> p q t", t=PACK),
+                in0=big[t][:].rearrange("p (q t) -> p q t", t=PACK),
+                scalar=fk_sb[:, t : t + 1],
+                in1=ra_ps[:].rearrange("p t q -> p q t"),
+                op0=ALU.mult,
+                op1=ALU.mult,
+            )
+            words = u_kj[t][:].bitcast(F32)
+            for u in range(2):
+                nc.tensor.transpose(u_ps[t][:, u, :], words[:, u : 2 * P : 2], ident[:])
+
+        def bring(t):
+            nc.scalar.copy(
+                out=u_jk[t][:].bitcast(F32).rearrange("p (m u) -> p m u", u=2),
+                in_=u_ps[t][:].rearrange("p u m -> p m u"),
+            )
+
+        def quant(t):
+            nc.vector.quantize_mx(out=u_w[t][:].bitcast(E5M2X4), scales=u_sc[t][:], in_=u_jk[t][:])
+            for h in range(2):
+                nc.tensor.matmul_mx(
+                    out=w_ps[h][:, t, :],
+                    lhsT=u_w[t][:].bitcast(E5M2X4),
+                    lhsT_scale=u_sc[t][:],
+                    rhs=gj_w[:, h * P : (h + 1) * P].bitcast(E5M2X4),
+                    rhs_scale=gj_sc[:, h * P : (h + 1) * P],
+                    start=True,
+                    stop=True,
+                )
+
+        gather_v(ga[0], 0, list_a, 0, 32)
+        gather_s(gb[0], 0, list_b, 0, 32)
+        gather_s(ga[1], 1, list_a, 0, 32)
+        gather_s(gb[1], 1, list_b, 0, 32)
+        combine(0)
+        weigh(0)
+        gather_v(ga[2], 2, list_a, 0, 32)
+        gather_s(gb[2], 2, list_b, 0, 32)
+        combine(1)
+        weigh(1)
+        bring(0)
+        gather_s(ga[3], 3, list_a, 0, 32)
+        combine(2)
+        weigh(2)
+        bring(1)
+        gather_s(gb[3], 3, list_b, 0, 16)
+        quant(0)
+        gather_v(gb[3], 3, list_b, 16, 32)
+        bring(2)
+        combine(3)
+        quant(1)
+        weigh(3)
+        quant(2)
+        bring(3)
+        quant(3)
+
+        w_bf = [keep.tile([P, P * PACK], BF16, name=f"w_bf{h}", align_bytes=64) for h in range(2)]
+        w_w = keep.tile([P, N], U32, name="w_w", align_bytes=64)
+        w_sc = keep.tile([P, N], U8, name="w_sc", align_bytes=64)
+        nc.scalar.copy(out=w_bf[0][:].rearrange("p (n t) -> p n t", t=PACK), in_=w_ps[0][:].rearrange("p t n -> p n t"))
+        nc.vector.tensor_copy(out=w_bf[1][:].rearrange("p (n t) -> p n t", t=PACK), in_=w_ps[1][:].rearrange("p t n -> p n t"))
+        for h in range(2):
+            nc.vector.quantize_mx(
+                out=w_w[:, h * P : (h + 1) * P].bitcast(E5M2X4), scales=w_sc[:, h * P : (h + 1) * P], in_=w_bf[h][:]
+            )
+
+        v_ps = [psum.tile([P, N], F32, name=f"v_ps{c}") for c in range(2)]
+        wv = [keep.tile([P, N], F32, name=f"wv{c}") for c in range(2)]
+        mag = [keep.tile([P, N], F32, name=f"mag{c}") for c in range(2)]
+        dw = [keep.tile([P, N], F32, name=f"dw{c}") for c in range(2)]
+        res = [keep.tile([P, N], F32, name=f"res{c}") for c in range(2)]
+        total = [keep.tile([P, 1], F32, name=f"total{c}") for c in range(2)]
+        spread = [keep.tile([P, 1], F32, name=f"spread{c}") for c in range(2)]
+        den = [keep.tile([P, 1], F32, name=f"den{c}") for c in range(2)]
+        rec = [keep.tile([P, 1], F32, name=f"rec{c}") for c in range(2)]
+        for c in range(2):
+            nc.tensor.matmul_mx(
+                out=v_ps[c][:],
+                lhsT=dr_w[:, 2 * c * P : 2 * (c + 1) * P].bitcast(E2M1X4),
+                lhsT_scale=dr_sc[:, c * P : (c + 1) * P],
+                rhs=w_w[:].bitcast(E5M2X4),
+                rhs_scale=w_sc[:],
+                start=True,
+                stop=True,
+            )
+        for c in range(2):
+            nc.vector.scalar_tensor_tensor(
+                out=wv[c][:], in0=v_ps[c][:], scalar=1.0, in1=bn_sb[:], op0=ALU.mult, op1=ALU.add, accum_out=total[c][:]
+            )
+        for c in range(2):
+            nc.scalar.activation(mag[c][:], wv[c][:], ACT.Abs, bias=total[c][:], scale=-float(N), accum_out=spread[c][:])
+        for c in range(2):
+            nc.vector.tensor_scalar(dw[c][:], wv[c][:], float(N), total[c][:], ALU.mult, ALU.subtract)
+        for c in range(2):
+            nc.vector.tensor_scalar(den[c][:], spread[c][:], 1.0 / N, 2.0 * N, ALU.mult, ALU.add)
+            nc.vector.reciprocal(rec[c][:], den[c][:])
+            nc.vector.tensor_scalar(res[c][:], dw[c][:], rec[c][:], None, ALU.mult)
+            nc.sync.dma_start(out=out[c * P : (c + 1) * P, :], in_=res[c][:])

@@ -32,24 +32,28 @@ def tile_list_directions_larger_stored_spread_kernel(
         list_a = keep.tile([P, J // 16], U16, name="list_a")
         list_b = keep.tile([P, J // 16], U16, name="list_b")
         rows = xf.rearrange("(p t) c -> t p c", t=PACK)
-        x_sb = [keep.tile([P, T], F32, name=f"x{t}") for t in range(PACK)]
+        x_sb = [keep.tile([P, T], F32, name=f"x{t}", tag=f"x{t}", align_bytes=64) for t in range(PACK)]
         ra_sb = keep.tile([P, PACK], F32, name="ra_sb")
         fk_sb = keep.tile([P, PACK], F32, name="fk_sb")
 
+        warm = keep.tile([P, 2], F32, name="warm")
+        nc.vector.memset(warm[:, 0:1], 1.0)
+        nc.scalar.activation(warm[:, 1:2], warm[:, 0:1], ACT.Abs_reciprocal_sqrt)
         nc.sync.dma_start(out=x_sb[0][:], in_=rows[0])
         nc.sync.dma_start(list_a[:], offs)
         nc.sync.dma_start(list_b[:], offs2)
-        nc.scalar.dma_start(out=ra_sb[:], in_=ra.rearrange("o (p t) -> (o p) t", t=PACK))
-        nc.scalar.dma_start(out=fk_sb[:], in_=fkr.rearrange("o (p t) -> (o p) t", t=PACK))
-        for t in range(1, PACK):
-            nc.sync.dma_start(out=x_sb[t][:], in_=rows[t])
+        nc.sync.dma_start(out=x_sb[1][:], in_=rows[1])
+        nc.sync.dma_start(out=x_sb[2][:], in_=rows[2])
+        nc.sync.dma_start(out=ra_sb[:], in_=ra.rearrange("o (p t) -> (o p) t", t=PACK))
+        nc.sync.dma_start(out=fk_sb[:], in_=fkr.rearrange("o (p t) -> (o p) t", t=PACK))
+        nc.sync.dma_start(out=x_sb[3][:], in_=rows[3])
 
         gj_sc = keep.tile([P, N], U8, name="gj_sc", align_bytes=64)
         dr_sc = keep.tile([P, R], U8, name="dr_sc", align_bytes=64)
-        nc.gpsimd.memset(gj_sc[:].bitcast(I32), 0)
-        nc.gpsimd.memset(dr_sc[:].bitcast(I32), 0)
         ident = keep.tile([P, P], F32, name="ident")
         make_identity(nc, ident[:])
+        nc.gpsimd.memset(gj_sc[:].bitcast(I32), 0)
+        nc.gpsimd.memset(dr_sc[:].bitcast(I32), 0)
 
         gj_w = keep.tile([P, N], U32, name="gj_w", align_bytes=64)
         dr_w = keep.tile([P, 2 * R], U8, name="dr_w", align_bytes=64)
@@ -66,82 +70,92 @@ def tile_list_directions_larger_stored_spread_kernel(
         for t in range(PACK):
             nc.tensor.transpose(ra_ps[:, t, :], ra_sb[:, t : t + 1].to_broadcast([P, P]), ident[:])
 
-        ga = [keep.tile([P, J], F32, name=f"ga{t}") for t in range(PACK)]
-        gb = [keep.tile([P, J], F32, name=f"gb{t}") for t in range(PACK)]
-        big = [keep.tile([P, J], F32, name=f"big{t}") for t in range(PACK)]
-        u_kj = [keep.tile([P, J], BF16, name=f"u_kj{t}") for t in range(PACK)]
-        u_ps = [psum.tile([P, 2, P], F32, name=f"u_ps{t}", tag=f"u_ps{t % 3}") for t in range(PACK)]
-        u_jk = [keep.tile([P, P * PACK], BF16, name=f"u_jk{t}", align_bytes=64) for t in range(PACK)]
-        u_w = [keep.tile([P, P], U32, name=f"u_w{t}", align_bytes=64) for t in range(PACK)]
-        u_sc = [keep.tile([P, P], U8, name=f"u_sc{t}", align_bytes=64) for t in range(PACK)]
+        u_kj = [keep.tile([P, J], BF16, name=f"u_kj{t}") for t in range(PACK - 1)]
+        u_half = [keep.tile([P, J // 2], BF16, name=f"u_half{u}") for u in range(2)]
+        u_ps01 = psum.tile([P, 2, 2, P], F32, name="u_ps01", tag="u_ps01")
+        u_ps2 = psum.tile([P, 1, 2, P], F32, name="u_ps2", tag="u_ps2")
+        u_ps3 = psum.tile([P, 1, 2, P], F32, name="u_ps3", tag="u_ps3")
+        u_ps = [u_ps01[:, 0], u_ps01[:, 1], u_ps2[:, 0], u_ps3[:, 0]]
         w_ps = [psum.tile([P, PACK, P], F32, name=f"w_ps{h}") for h in range(2)]
+        split = [0, 0, 32, 20]
 
-        def gather_v(dst, t, lst, c0, c1):
-            nc.vector.tensor_copy(dst[:, 16 * c0 : 16 * c1], x_sb[t][:].indirect(lst[:, c0:c1]))
+        ga, gb, big = {}, {}, {}
+        cut = 8
 
-        def gather_s(dst, t, lst, c0, c1):
-            nc.scalar.activation(dst[:, 16 * c0 : 16 * c1], x_sb[t][:].indirect(lst[:, c0:c1]), ACT.Copy)
+        def gather(t):
+            ga[t] = keep.tile([P, J], F32, name=f"ga{t}", tag=f"ga{t % 2}", align_bytes=64)
+            gb[t] = keep.tile([P, J], F32, name=f"gb{t}", tag=("gb0", "gb1", "gb2", "big1")[t], align_bytes=64)
+            c = split[t]
+            first = cut if t == PACK - 1 else 0
+            nc.scalar.activation(ga[t][:], x_sb[t][:].indirect(list_a[:]), ACT.Copy)
+            for c0, c1 in ((first, c), (0, first)):
+                if c1 > c0:
+                    nc.scalar.activation(gb[t][:, 16 * c0 : 16 * c1], x_sb[t][:].indirect(list_b[:, c0:c1]), ACT.Copy)
+            if c < J // 16:
+                nc.vector.tensor_copy(gb[t][:, 16 * c :], x_sb[t][:].indirect(list_b[:, c:]))
 
-        def combine(t):
-            nc.vector.tensor_tensor(big[t][:], ga[t][:], gb[t][:], ALU.max)
+        def parts(t):
+            return [(0, J)] if t < PACK - 1 else [(16 * cut, J), (0, 16 * cut)]
+
+        def larger(t):
+            big[t] = keep.tile([P, J], F32, name=f"big{t}", tag=("big0", "big1", "big0", "big3")[t], align_bytes=64)
+            for j0, j1 in parts(t):
+                nc.vector.tensor_tensor(big[t][:, j0:j1], ga[t][:, j0:j1], gb[t][:, j0:j1], ALU.max)
 
         def weigh(t):
-            nc.vector.scalar_tensor_tensor(
-                out=u_kj[t][:].rearrange("p (q t) -> p q t", t=PACK),
-                in0=big[t][:].rearrange("p (q t) -> p q t", t=PACK),
-                scalar=fk_sb[:, t : t + 1],
-                in1=ra_ps[:].rearrange("p t q -> p q t"),
-                op0=ALU.mult,
-                op1=ALU.mult,
-            )
-            words = u_kj[t][:].bitcast(F32)
-            for u in range(2):
-                nc.tensor.transpose(u_ps[t][:, u, :], words[:, u : 2 * P : 2], ident[:])
-
-        def bring(t):
-            nc.scalar.copy(
-                out=u_jk[t][:].bitcast(F32).rearrange("p (m u) -> p m u", u=2),
-                in_=u_ps[t][:].rearrange("p u m -> p m u"),
-            )
-
-        def quant(t):
-            nc.vector.quantize_mx(out=u_w[t][:].bitcast(E5M2X4), scales=u_sc[t][:], in_=u_jk[t][:])
-            for h in range(2):
-                nc.tensor.matmul_mx(
-                    out=w_ps[h][:, t, :],
-                    lhsT=u_w[t][:].bitcast(E5M2X4),
-                    lhsT_scale=u_sc[t][:],
-                    rhs=gj_w[:, h * P : (h + 1) * P].bitcast(E5M2X4),
-                    rhs_scale=gj_sc[:, h * P : (h + 1) * P],
-                    start=True,
-                    stop=True,
+            if t < PACK - 1:
+                words = u_kj[t][:].bitcast(F32)
+                nc.vector.scalar_tensor_tensor(
+                    out=u_kj[t][:].rearrange("p (q t) -> p q t", t=PACK),
+                    in0=big[t][:].rearrange("p (q t) -> p q t", t=PACK),
+                    scalar=fk_sb[:, t : t + 1],
+                    in1=ra_ps[:].rearrange("p t q -> p q t"),
+                    op0=ALU.mult,
+                    op1=ALU.mult,
                 )
+                for u in range(2):
+                    nc.tensor.transpose(u_ps[t][:, u, :], words[:, u : 2 * P : 2], ident[:])
+                return
+            for u in range(2):
+                for j0, j1 in parts(t):
+                    q0, q1 = j0 // PACK, j1 // PACK
+                    nc.vector.scalar_tensor_tensor(
+                        out=u_half[u][:, 2 * q0 : 2 * q1].rearrange("p (q e) -> p q e", e=2),
+                        in0=big[t][:, j0:j1].rearrange("p (q t) -> p q t", t=PACK)[:, :, 2 * u : 2 * u + 2],
+                        scalar=fk_sb[:, t : t + 1],
+                        in1=ra_ps[:, 2 * u : 2 * u + 2, q0:q1].rearrange("p e q -> p q e"),
+                        op0=ALU.mult,
+                        op1=ALU.mult,
+                    )
+                nc.tensor.transpose(u_ps[t][:, u, :], u_half[u][:].bitcast(F32), ident[:])
 
-        gather_v(ga[0], 0, list_a, 0, 32)
-        gather_s(gb[0], 0, list_b, 0, 32)
-        gather_s(ga[1], 1, list_a, 0, 32)
-        gather_s(gb[1], 1, list_b, 0, 32)
-        combine(0)
-        weigh(0)
-        gather_v(ga[2], 2, list_a, 0, 32)
-        gather_s(gb[2], 2, list_b, 0, 32)
-        combine(1)
-        weigh(1)
-        bring(0)
-        gather_s(ga[3], 3, list_a, 0, 32)
-        combine(2)
-        weigh(2)
-        bring(1)
-        gather_s(gb[3], 3, list_b, 0, 16)
-        quant(0)
-        gather_v(gb[3], 3, list_b, 16, 32)
-        bring(2)
-        combine(3)
-        quant(1)
-        weigh(3)
-        quant(2)
-        bring(3)
-        quant(3)
+        gather(0)
+        for t in range(PACK):
+            larger(t)
+            if t + 1 < PACK:
+                gather(t + 1)
+            weigh(t)
+
+        for t0, n, bank, tag_in, tag_out in ((0, 2, u_ps01, "x3", "big3"), (2, 1, u_ps2, "ga1", "u_w2"), (3, 1, u_ps3, "u_jk3", "u_w3")):
+            u_jk = keep.tile([P, n * P * PACK], BF16, name=f"u_jk{t0}", tag=tag_in, align_bytes=64)
+            u_w = keep.tile([P, n * P], U32, name=f"u_w{t0}", tag=tag_out, align_bytes=64)
+            u_sc = keep.tile([P, n * P], U8, name=f"u_sc{t0}", align_bytes=64)
+            nc.scalar.copy(
+                out=u_jk[:].bitcast(F32).rearrange("p (i m u) -> p i m u", u=2, i=n),
+                in_=bank[:].rearrange("p i u m -> p i m u"),
+            )
+            nc.vector.quantize_mx(out=u_w[:].bitcast(E5M2X4), scales=u_sc[:], in_=u_jk[:])
+            for i in range(n):
+                for h in range(2):
+                    nc.tensor.matmul_mx(
+                        out=w_ps[h][:, t0 + i, :],
+                        lhsT=u_w[:, i * P : (i + 1) * P].bitcast(E5M2X4),
+                        lhsT_scale=u_sc[:, i * P : (i + 1) * P],
+                        rhs=gj_w[:, h * P : (h + 1) * P].bitcast(E5M2X4),
+                        rhs_scale=gj_sc[:, h * P : (h + 1) * P],
+                        start=True,
+                        stop=True,
+                    )
 
         w_bf = [keep.tile([P, P * PACK], BF16, name=f"w_bf{h}", align_bytes=64) for h in range(2)]
         w_w = keep.tile([P, N], U32, name="w_w", align_bytes=64)
@@ -160,18 +174,18 @@ def tile_list_directions_larger_stored_spread_kernel(
         res = [keep.tile([P, N], F32, name=f"res{c}") for c in range(2)]
         total = [keep.tile([P, 1], F32, name=f"total{c}") for c in range(2)]
         spread = [keep.tile([P, 1], F32, name=f"spread{c}") for c in range(2)]
-        den = [keep.tile([P, 1], F32, name=f"den{c}") for c in range(2)]
         rec = [keep.tile([P, 1], F32, name=f"rec{c}") for c in range(2)]
-        for c in range(2):
-            nc.tensor.matmul_mx(
-                out=v_ps[c][:],
-                lhsT=dr_w[:, 2 * c * P : 2 * (c + 1) * P].bitcast(E2M1X4),
-                lhsT_scale=dr_sc[:, c * P : (c + 1) * P],
-                rhs=w_w[:].bitcast(E5M2X4),
-                rhs_scale=w_sc[:],
-                start=True,
-                stop=True,
-            )
+        for h in range(2):
+            for c in range(2):
+                nc.tensor.matmul_mx(
+                    out=v_ps[c][:, h * P : (h + 1) * P],
+                    lhsT=dr_w[:, 2 * c * P : 2 * (c + 1) * P].bitcast(E2M1X4),
+                    lhsT_scale=dr_sc[:, c * P : (c + 1) * P],
+                    rhs=w_w[:, h * P : (h + 1) * P].bitcast(E5M2X4),
+                    rhs_scale=w_sc[:, h * P : (h + 1) * P],
+                    start=True,
+                    stop=True,
+                )
         for c in range(2):
             nc.vector.scalar_tensor_tensor(
                 out=wv[c][:], in0=v_ps[c][:], scalar=1.0, in1=bn_sb[:], op0=ALU.mult, op1=ALU.add, accum_out=total[c][:]
@@ -181,7 +195,6 @@ def tile_list_directions_larger_stored_spread_kernel(
         for c in range(2):
             nc.vector.tensor_scalar(dw[c][:], wv[c][:], float(N), total[c][:], ALU.mult, ALU.subtract)
         for c in range(2):
-            nc.vector.tensor_scalar(den[c][:], spread[c][:], 1.0 / N, 2.0 * N, ALU.mult, ALU.add)
-            nc.vector.reciprocal(rec[c][:], den[c][:])
-            nc.vector.tensor_scalar(res[c][:], dw[c][:], rec[c][:], None, ALU.mult)
+            nc.scalar.activation(rec[c][:], spread[c][:], ACT.Abs_reciprocal_sqrt, bias=2.0 * N, scale=1.0 / N)
+            nc.vector.tensor_scalar(res[c][:], dw[c][:], rec[c][:], rec[c][:], ALU.mult, ALU.mult)
             nc.sync.dma_start(out=out[c * P : (c + 1) * P, :], in_=res[c][:])

from contextlib import ExitStack

import concourse.mybir as mybir
from concourse.masks import make_identity

K, J, N, R, T = 512, 512, 256, 256, 1024
FLOPS = 2 * J * K * N + 2 * K * R * N

F32 = mybir.dt.float32
BF16 = mybir.dt.bfloat16
I32 = mybir.dt.int32
U32 = mybir.dt.uint32
U16 = mybir.dt.uint16
U8 = mybir.dt.uint8
E5M2X4 = mybir.dt.float8_e5m2_x4
E2M1X4 = mybir.dt.float4_e2m1fn_x4
ALU = mybir.AluOpType
ACT = mybir.ActivationFunctionType

P = 128
PACK = 4


def tile_list_directions_larger_stored_spread_kernel(
    tc, xf, ra, gj_words, gj_scales, fkr, dr_words, dr_scales, bn, offs, offs2, out
):
    nc = tc.nc
    with ExitStack() as ctx:
        keep = ctx.enter_context(tc.tile_pool(name="keep", bufs=1))
        psum = ctx.enter_context(tc.psum_pool(name="psum", bufs=1))

        list_a = keep.tile([P, J // 16], U16, name="list_a")
        list_b = keep.tile([P, J // 16], U16, name="list_b")
        rows = xf.rearrange("(p t) c -> t p c", t=PACK)
        x_sb = [keep.tile([P, T], F32, name=f"x{t}", tag=f"x{t}", align_bytes=64) for t in range(PACK)]
        ra_sb = keep.tile([P, PACK], F32, name="ra_sb")
        fk_sb = keep.tile([P, PACK], F32, name="fk_sb")

        warm = keep.tile([P, 2], F32, name="warm")
        nc.vector.memset(warm[:, 0:1], 1.0)
        nc.scalar.activation(warm[:, 1:2], warm[:, 0:1], ACT.Abs_reciprocal_sqrt)
        nc.sync.dma_start(out=x_sb[0][:], in_=rows[0])
        nc.sync.dma_start(list_a[:], offs)
        nc.sync.dma_start(list_b[:], offs2)
        nc.sync.dma_start(out=x_sb[1][:], in_=rows[1])
        nc.sync.dma_start(out=x_sb[2][:], in_=rows[2])
        nc.sync.dma_start(out=ra_sb[:], in_=ra.rearrange("o (p t) -> (o p) t", t=PACK))
        nc.sync.dma_start(out=fk_sb[:], in_=fkr.rearrange("o (p t) -> (o p) t", t=PACK))
        nc.sync.dma_start(out=x_sb[3][:], in_=rows[3])

        gj_sc = keep.tile([P, N], U8, name="gj_sc", align_bytes=64)
        dr_sc = keep.tile([P, R], U8, name="dr_sc", align_bytes=64)
        ident = keep.tile([P, P], F32, name="ident")
        make_identity(nc, ident[:])
        nc.gpsimd.memset(gj_sc[:].bitcast(I32), 0)
        nc.gpsimd.memset(dr_sc[:].bitcast(I32), 0)

        gj_w = keep.tile([P, N], U32, name="gj_w", align_bytes=64)
        dr_w = keep.tile([P, 2 * R], U8, name="dr_w", align_bytes=64)
        bn_sb = keep.tile([P, N], F32, name="bn_sb")
        nc.sync.dma_start(out=gj_w[:].bitcast(I32), in_=gj_words[0].rearrange("p n t -> p (n t)").bitcast(I32))
        for q in range(4):
            nc.sync.dma_start(out=gj_sc[32 * q : 32 * q + 4, :].bitcast(I32), in_=gj_scales[0, 4 * q : 4 * q + 4, :].bitcast(I32))
        nc.sync.dma_start(out=dr_w[:].bitcast(I32), in_=dr_words[0].bitcast(I32))
        for q in range(4):
            nc.sync.dma_start(out=dr_sc[32 * q : 32 * q + 4, :].bitcast(I32), in_=dr_scales[0, 4 * q : 4 * q + 4, :].bitcast(I32))
        nc.sync.dma_start(out=bn_sb[:], in_=bn[0].partition_broadcast(P))

        ra_ps = psum.tile([P, PACK, P], F32, name="ra_ps")
        for t in range(PACK):
            nc.tensor.transpose(ra_ps[:, t, :], ra_sb[:, t : t + 1].to_broadcast([P, P]), ident[:])

        u_kj = [keep.tile([P, J], BF16, name=f"u_kj{t}") for t in range(PACK - 1)]
        u_half = [keep.tile([P, J // 2], BF16, name=f"u_half{u}") for u in range(2)]
        u_ps01 = psum.tile([P, 2, 2, P], F32, name="u_ps01", tag="u_ps01")
        u_ps2 = psum.tile([P, 1, 2, P], F32, name="u_ps2", tag="u_ps2")
        u_ps3 = psum.tile([P, 1, 2, P], F32, name="u_ps3", tag="u_ps3")
        u_ps = [u_ps01[:, 0], u_ps01[:, 1], u_ps2[:, 0], u_ps3[:, 0]]
        w_ps = [psum.tile([P, PACK, P], F32, name=f"w_ps{h}") for h in range(2)]
        split = [0, 0, 32, 20]

        ga, gb, big = {}, {}, {}
        cut = 8

        def gather(t):
            ga[t] = keep.tile([P, J], F32, name=f"ga{t}", tag=f"ga{t % 2}", align_bytes=64)
            gb[t] = keep.tile([P, J], F32, name=f"gb{t}", tag=("gb0", "gb1", "gb2", "big1")[t], align_bytes=64)
            c = split[t]
            first = cut if t == PACK - 1 else 0
            nc.scalar.activation(ga[t][:], x_sb[t][:].indirect(list_a[:]), ACT.Copy)
            for c0, c1 in ((first, c), (0, first)):
                if c1 > c0:
                    nc.scalar.activation(gb[t][:, 16 * c0 : 16 * c1], x_sb[t][:].indirect(list_b[:, c0:c1]), ACT.Copy)
            if c < J // 16:
                nc.vector.tensor_copy(gb[t][:, 16 * c :], x_sb[t][:].indirect(list_b[:, c:]))

        def parts(t):
            return [(0, J)] if t < PACK - 1 else [(16 * cut, J), (0, 16 * cut)]

        def larger(t):
            big[t] = keep.tile([P, J], F32, name=f"big{t}", tag=("big0", "big1", "big0", "big3")[t], align_bytes=64)
            for j0, j1 in parts(t):
                nc.vector.tensor_tensor(big[t][:, j0:j1], ga[t][:, j0:j1], gb[t][:, j0:j1], ALU.max)

        def weigh(t):
            if t < PACK - 1:
                words = u_kj[t][:].bitcast(F32)
                nc.vector.scalar_tensor_tensor(
                    out=u_kj[t][:].rearrange("p (q t) -> p q t", t=PACK),
                    in0=big[t][:].rearrange("p (q t) -> p q t", t=PACK),
                    scalar=fk_sb[:, t : t + 1],
                    in1=ra_ps[:].rearrange("p t q -> p q t"),
                    op0=ALU.mult,
                    op1=ALU.mult,
                )
                for u in range(2):
                    nc.tensor.transpose(u_ps[t][:, u, :], words[:, u : 2 * P : 2], ident[:])
                return
            for u in range(2):
                for j0, j1 in parts(t):
                    q0, q1 = j0 // PACK, j1 // PACK
                    nc.vector.scalar_tensor_tensor(
                        out=u_half[u][:, 2 * q0 : 2 * q1].rearrange("p (q e) -> p q e", e=2),
                        in0=big[t][:, j0:j1].rearrange("p (q t) -> p q t", t=PACK)[:, :, 2 * u : 2 * u + 2],
                        scalar=fk_sb[:, t : t + 1],
                        in1=ra_ps[:, 2 * u : 2 * u + 2, q0:q1].rearrange("p e q -> p q e"),
                        op0=ALU.mult,
                        op1=ALU.mult,
                    )
                nc.tensor.transpose(u_ps[t][:, u, :], u_half[u][:].bitcast(F32), ident[:])

        gather(0)
        for t in range(PACK):
            larger(t)
            if t + 1 < PACK:
                gather(t + 1)
            weigh(t)

        for t0, n, bank, tag_in, tag_out in ((0, 2, u_ps01, "x3", "big3"), (2, 1, u_ps2, "ga1", "u_w2"), (3, 1, u_ps3, "u_jk3", "u_w3")):
            u_jk = keep.tile([P, n * P * PACK], BF16, name=f"u_jk{t0}", tag=tag_in, align_bytes=64)
            u_w = keep.tile([P, n * P], U32, name=f"u_w{t0}", tag=tag_out, align_bytes=64)
            u_sc = keep.tile([P, n * P], U8, name=f"u_sc{t0}", align_bytes=64)
            nc.scalar.copy(
                out=u_jk[:].bitcast(F32).rearrange("p (i m u) -> p i m u", u=2, i=n),
                in_=bank[:].rearrange("p i u m -> p i m u"),
            )
            nc.vector.quantize_mx(out=u_w[:].bitcast(E5M2X4), scales=u_sc[:], in_=u_jk[:])
            for i in range(n):
                for h in range(2):
                    nc.tensor.matmul_mx(
                        out=w_ps[h][:, t0 + i, :],
                        lhsT=u_w[:, i * P : (i + 1) * P].bitcast(E5M2X4),
                        lhsT_scale=u_sc[:, i * P : (i + 1) * P],
                        rhs=gj_w[:, h * P : (h + 1) * P].bitcast(E5M2X4),
                        rhs_scale=gj_sc[:, h * P : (h + 1) * P],
                        start=True,
                        stop=True,
                    )

        w_bf = [keep.tile([P, P * PACK], BF16, name=f"w_bf{h}", align_bytes=64) for h in range(2)]
        w_w = keep.tile([P, N], U32, name="w_w", align_bytes=64)
        w_sc = keep.tile([P, N], U8, name="w_sc", align_bytes=64)
        nc.scalar.copy(out=w_bf[0][:].rearrange("p (n t) -> p n t", t=PACK), in_=w_ps[0][:].rearrange("p t n -> p n t"))
        nc.vector.tensor_copy(out=w_bf[1][:].rearrange("p (n t) -> p n t", t=PACK), in_=w_ps[1][:].rearrange("p t n -> p n t"))
        for h in range(2):
            nc.vector.quantize_mx(
                out=w_w[:, h * P : (h + 1) * P].bitcast(E5M2X4), scales=w_sc[:, h * P : (h + 1) * P], in_=w_bf[h][:]
            )

        v_ps = [psum.tile([P, N], F32, name=f"v_ps{c}") for c in range(2)]
        wv = [keep.tile([P, N], F32, name=f"wv{c}") for c in range(2)]
        mag = [keep.tile([P, N], F32, name=f"mag{c}") for c in range(2)]
        dw = [keep.tile([P, N], F32, name=f"dw{c}") for c in range(2)]
        res = [keep.tile([P, N], F32, name=f"res{c}") for c in range(2)]
        total = [keep.tile([P, 1], F32, name=f"total{c}") for c in range(2)]
        spread = [keep.tile([P, 1], F32, name=f"spread{c}") for c in range(2)]
        rec = [keep.tile([P, 1], F32, name=f"rec{c}") for c in range(2)]
        for h in range(2):
            for c in range(2):
                nc.tensor.matmul_mx(
                    out=v_ps[c][:, h * P : (h + 1) * P],
                    lhsT=dr_w[:, 2 * c * P : 2 * (c + 1) * P].bitcast(E2M1X4),
                    lhsT_scale=dr_sc[:, c * P : (c + 1) * P],
                    rhs=w_w[:, h * P : (h + 1) * P].bitcast(E5M2X4),
                    rhs_scale=w_sc[:, h * P : (h + 1) * P],
                    start=True,
                    stop=True,
                )
        for c in range(2):
            nc.vector.scalar_tensor_tensor(
                out=wv[c][:], in0=v_ps[c][:], scalar=1.0, in1=bn_sb[:], op0=ALU.mult, op1=ALU.add, accum_out=total[c][:]
            )
        for c in range(2):
            nc.scalar.activation(mag[c][:], wv[c][:], ACT.Abs, bias=total[c][:], scale=-float(N), accum_out=spread[c][:])
        for c in range(2):
            nc.vector.tensor_scalar(dw[c][:], wv[c][:], float(N), total[c][:], ALU.mult, ALU.subtract)
        for c in range(2):
            nc.scalar.activation(rec[c][:], spread[c][:], ACT.Abs_reciprocal_sqrt, bias=2.0 * N, scale=1.0 / N)
            nc.vector.tensor_scalar(res[c][:], dw[c][:], rec[c][:], rec[c][:], ALU.mult, ALU.mult)
            nc.sync.dma_start(out=out[c * P : (c + 1) * P, :], in_=res[c][:])
